import numpy as np
import ml_dtypes


def mxq(x, axis, fmt="e4m3"):
    dtype, down = {"e4m3": (ml_dtypes.float8_e4m3fn, 7), "e5m2": (ml_dtypes.float8_e5m2, 14)}[fmt]
    v = np.moveaxis(np.asarray(x, np.float32).astype(ml_dtypes.bfloat16).astype(np.float64), axis, -1)
    blocks = v.reshape(v.shape[:-1] + (-1, 32))
    amax = np.abs(blocks).max(-1, keepdims=True)
    byte = np.maximum(np.where(amax > 0, np.frexp(amax)[1] - 1 + 127, 0) - down, 1)
    scale = np.exp2(byte - 127.0)
    codes = (blocks / scale).astype(np.float32).astype(dtype).astype(np.float64)
    return np.moveaxis((codes * scale).reshape(v.shape), -1, axis)


WIDE = False


def mx_kscale(k):
    if not WIDE:
        return np.ones(k)
    levels = np.array([10, -10, 5, -5, 0])
    if k % 512:
        return np.exp2(np.random.permutation(np.resize(levels, k // 32))).repeat(32)
    a = np.empty((k // 512, 16))
    for p in range(k // 512):
        a[p, :8] = np.random.permutation(np.resize(levels, 8))
        for g in range(8):
            far = levels[np.abs(levels - a[p, g]) >= 10]
            a[p, g + 8] = far[np.random.randint(len(far))]
    return np.exp2(a.ravel()).repeat(32)


def f64(x):
    return np.asarray(x).astype(np.float64)


def striped8(idx):
    return np.asarray(idx).reshape(8, -1, 16).transpose(0, 2, 1).reshape(128, -1).astype(np.uint16)


def unstriped8(offs):
    return offs.reshape(8, 16, -1).transpose(0, 2, 1).reshape(8, -1).astype(np.int64)


def pick8(x, idx, run):
    r = np.arange(len(x))
    return x[r[:, None], idx[r % (8 * run) // run]]


E2M1 = np.array([0.0, 0.5, 1.0, 1.5, 2.0, 3.0, 4.0, 6.0, -0.0, -0.5, -1.0, -1.5, -2.0, -3.0, -4.0, -6.0])


def pack_weight(w, fmt):
    k, n = w.shape
    w = f64(np.asarray(w, np.float32).astype(ml_dtypes.bfloat16)).reshape(k // 32, 32, n)
    amax = np.abs(w).max(1)
    if fmt == "e4m3":
        byte = np.frexp(amax)[1] - 1 + 127 - 7
    else:
        mant, ex = np.frexp(amax / 6.0)
        byte = np.where(mant > 0.5, ex, ex - 1) + 127
    byte = np.clip(np.where(amax > 0, byte, 1), 1, 254)
    scaled = (w * np.exp2(127.0 - byte)[:, None, :]).reshape(k, n).astype(np.float32)
    by_word = np.ascontiguousarray(scaled.reshape(k // 512, 128, 4, n).transpose(0, 1, 3, 2))
    if fmt == "e4m3":
        words = by_word.astype(ml_dtypes.float8_e4m3fn).view(np.uint8)
    else:
        c = by_word.astype(ml_dtypes.float4_e2m1fn).view(np.uint8) & 0xF
        words = (c[..., 0::2] | (c[..., 1::2] << 4)).reshape(k // 512, 128, 2 * n)
    return np.ascontiguousarray(words), np.ascontiguousarray(byte.astype(np.uint8).reshape(k // 512, 16, n))


def unpack_weight(words, scales, fmt):
    g, _, n = scales.shape
    words = np.ascontiguousarray(words).reshape(g, 128, n, -1)
    if fmt == "e4m3":
        vals = words.view(ml_dtypes.float8_e4m3fn).astype(np.float64)
    else:
        nib = np.empty((g, 128, n, 4), np.uint8)
        nib[..., 0::2] = words & 0xF
        nib[..., 1::2] = words >> 4
        vals = E2M1[nib]
    vals = vals * np.repeat(np.exp2(scales.astype(np.float64) - 127.0), 8, axis=1)[..., None]
    return vals.transpose(0, 1, 3, 2).reshape(g * 512, n)


D, K, T, I, J, Q = 512, 512, 1024, 512, 256, 128


def setup_inputs():
    n = np.random.standard_normal
    idx = np.stack([np.random.permutation(T)[:J] for _ in range(8)])
    idx2 = np.stack([np.random.permutation(T)[:J] for _ in range(8)])
    idx3 = np.stack([np.random.permutation(T)[:I] for _ in range(8)])
    idx4 = np.stack([np.random.permutation(T)[:J] for _ in range(8)])
    idx5 = np.stack([np.random.permutation(T)[:I] for _ in range(8)])
    fd = mx_kscale(D)
    fk = mx_kscale(K)
    wqp = pack_weight(n((D, K)) * 1.0 / np.sqrt(D) * fd[:, None] * fk, "e4m3")
    cachep = pack_weight(n((K, T)) * 1.0 / np.sqrt(K) / fk[:, None], "e2m1")
    tagsp = pack_weight(n((D, T)) * 0.5 / np.sqrt(D) * fd[:, None], "e4m3")
    return {
        "states": (n((D, Q)) * 0.95 / fd[:, None]).astype(np.float32),
        "wq_words": wqp[0],
        "wq_scales": wqp[1],
        "cache_words": cachep[0],
        "cache_scales": cachep[1],
        "tags_words": tagsp[0],
        "tags_scales": tagsp[1],
        "offs": striped8(idx),
        "offs2": striped8(idx2),
        "offs3": striped8(idx3),
        "offs4": striped8(idx4),
        "offs5": striped8(idx5),
    }


def reference(states, wq_words, wq_scales, cache_words, cache_scales, tags_words, tags_scales, offs, offs2, offs3, offs4, offs5):
    idx = unstriped8(offs)
    idx2 = unstriped8(offs2)
    idx3 = unstriped8(offs3)
    idx4 = unstriped8(offs4)
    idx5 = unstriped8(offs5)
    wqu = unpack_weight(wq_words, wq_scales, "e4m3")
    cacheu = unpack_weight(cache_words, cache_scales, "e2m1")
    tagsu = unpack_weight(tags_words, tags_scales, "e4m3")
    statesq = mxq(f64(states), 0, "e4m3")
    qv = wqu.T @ statesq
    qvq = mxq(qv, 0, "e4m3")
    a = qvq.T @ cacheu + statesq.T @ tagsu
    w = np.concatenate([pick8(a, idx, 16), pick8(a, idx2, 16)], axis=1)
    f1 = np.zeros((Q, T))
    f1[np.arange(Q)[:, None], idx3[np.arange(Q) % 128 // 16]] = w
    c1 = a - f1
    v = pick8(c1, idx4, 16) - pick8(a, idx, 16)
    f2 = np.zeros((Q, T))
    f2[np.arange(Q)[:, None], idx2[np.arange(Q) % 128 // 16]] = v
    c2 = np.maximum(c1, f2)
    y = pick8(c2, idx5, 16)
    return y

@@ -1,0 +1,177 @@
+from contextlib import ExitStack
+
+import concourse.mybir as mybir
+
+D, K, T, I, J, Q = 512, 512, 1024, 512, 256, 128
+FLOPS = 2 * D * K * Q + 2 * K * T * Q + 2 * D * T * Q
+
+F32 = mybir.dt.float32
+BF16 = mybir.dt.bfloat16
+I32 = mybir.dt.int32
+U32 = mybir.dt.uint32
+U16 = mybir.dt.uint16
+U8 = mybir.dt.uint8
+FP8X4 = mybir.dt.float8_e4m3fn_x4
+FP4X4 = mybir.dt.float4_e2m1fn_x4
+COPY = mybir.ActivationFunctionType.Copy
+SUB = mybir.AluOpType.subtract
+MAX = mybir.AluOpType.max
+
+P = 128
+PACK = 4
+CHUNK = 256
+CAST_SPLIT = 64
+
+
+def tile_attend_halfruns_parts_kernel(
+    tc, states, wq_words, wq_scales, cache_words, cache_scales, tags_words, tags_scales,
+    offs, offs2, offs3, offs4, offs5, out,
+):
+    nc = tc.nc
+    with ExitStack() as ctx:
+        lists = ctx.enter_context(tc.tile_pool(name="lists", bufs=1))
+        sb = ctx.enter_context(tc.tile_pool(name="sb", bufs=1))
+        psum = ctx.enter_context(tc.psum_pool(name="psum", bufs=1))
+
+        def load_scale_rows(scales, width, name):
+            rows = sb.tile([PACK, 4, width // 4], I32, name=name, align_bytes=64)
+            nc.sync.dma_start(rows[:], scales[0].bitcast(I32).rearrange("(g r) n -> r g n", r=PACK))
+            return rows
+
+        def spread_scale_rows(rows, plane):
+            for g in range(4):
+                nc.vector.tensor_copy(plane[32 * g : 32 * g + PACK, :].bitcast(I32), rows[:, g, :])
+
+        wq_plane = sb.tile([P, K], U8, align_bytes=64)
+        tags_plane = sb.tile([P, T], U8, align_bytes=64)
+        cache_plane = sb.tile([P, T], U8, align_bytes=64)
+        for plane in (wq_plane, tags_plane, cache_plane):
+            nc.vector.memset(plane[:].bitcast(I32), 0)
+        f1 = sb.tile([P, T], F32, align_bytes=64)
+        f2 = sb.tile([P, T], F32, align_bytes=64)
+        nc.vector.memset(f1[:], 0.0)
+        nc.vector.memset(f2[:], 0.0)
+
+        wq_rows = load_scale_rows(wq_scales, K, "wq_rows")
+        st_raw = sb.tile([P, PACK, Q], F32, align_bytes=64)
+        nc.sync.dma_start(st_raw[:], states.rearrange("(p j) q -> p j q", j=PACK))
+        wq_raw = sb.tile([P, K], U32, align_bytes=64)
+        nc.sync.dma_start(wq_raw[:].bitcast(I32), wq_words[0].rearrange("p n t -> p (n t)").bitcast(I32))
+        tags_rows = load_scale_rows(tags_scales, T, "tags_rows")
+        cache_rows = load_scale_rows(cache_scales, T, "cache_rows")
+        tags_codes = sb.tile([P, T], U32, align_bytes=64)
+        nc.sync.dma_start(tags_codes[:].bitcast(I32), tags_words[0].rearrange("p n t -> p (n t)").bitcast(I32))
+        cache_codes = sb.tile([P, 2 * T], U8, align_bytes=64)
+        nc.sync.dma_start(cache_codes[:].bitcast(I32), cache_words[0].bitcast(I32))
+        l1 = lists.tile([P, J // 16], U16)
+        l2 = lists.tile([P, J // 16], U16)
+        l3 = lists.tile([P, I // 16], U16)
+        l4 = lists.tile([P, J // 16], U16)
+        l5 = lists.tile([P, I // 16], U16)
+        for tile_, src in ((l1, offs), (l2, offs2), (l3, offs3), (l4, offs4), (l5, offs5)):
+            nc.sync.dma_start(tile_[:], src)
+
+        spread_scale_rows(wq_rows, wq_plane)
+
+        st_bf = sb.tile([P, Q, PACK], BF16, align_bytes=64)
+        nc.scalar.activation(
+            st_bf[:, CAST_SPLIT:, :].rearrange("p (c i) j -> p c j i", i=4),
+            st_raw[:, :, CAST_SPLIT:].rearrange("p j (c i) -> p c j i", i=4),
+            COPY,
+        )
+        nc.vector.tensor_copy(
+            st_bf[:, :CAST_SPLIT, :].rearrange("p (c i) j -> p c j i", i=4),
+            st_raw[:, :, :CAST_SPLIT].rearrange("p j (c i) -> p c j i", i=4),
+        )
+
+        wq_dealt_plane = sb.tile([P, K], U8, align_bytes=64)
+        nc.vector.tensor_copy(
+            wq_dealt_plane[:].rearrange("p (t m) -> p t m", t=PACK),
+            wq_plane[:].rearrange("p (m t) -> p t m", t=PACK),
+        )
+        wq_dealt = sb.tile([P, K], U32, align_bytes=64)
+        nc.scalar.copy(
+            wq_dealt[:].rearrange("p (t b i) -> p b t i", t=PACK, i=4),
+            wq_raw[:].rearrange("p (b i t) -> p b t i", t=PACK, i=4),
+        )
+
+        st_codes = sb.tile([P, Q], U32, align_bytes=64)
+        st_plane = sb.tile([P, Q], U8, align_bytes=64)
+        nc.vector.quantize_mx(
+            out=st_codes[:].bitcast(FP8X4), scales=st_plane[:], in_=st_bf[:].rearrange("p q j -> p (q j)")
+        )
+
+        qv_ps = psum.tile([P, PACK, Q], F32)
+        for t in range(PACK):
+            cols = slice(t * P, (t + 1) * P)
+            nc.tensor.matmul_mx(
+                out=qv_ps[:, t, :],
+                lhsT=wq_dealt[:, cols].bitcast(FP8X4),
+                lhsT_scale=wq_dealt_plane[:, cols],
+                rhs=st_codes[:].bitcast(FP8X4),
+                rhs_scale=st_plane[:],
+                start=True,
+                stop=True,
+            )
+
+        spread_scale_rows(tags_rows, tags_plane)
+        spread_scale_rows(cache_rows, cache_plane)
+
+        banks = [psum.tile([P, CHUNK], F32, name="bank%d" % c) for c in range(T // CHUNK)]
+        for c, bank in enumerate(banks):
+            cols = slice(c * CHUNK, (c + 1) * CHUNK)
+            nc.tensor.matmul_mx(
+                out=bank[:],
+                lhsT=st_codes[:].bitcast(FP8X4),
+                lhsT_scale=st_plane[:],
+                rhs=tags_codes[:, cols].bitcast(FP8X4),
+                rhs_scale=tags_plane[:, cols],
+                start=True,
+                stop=False,
+            )
+
+        qv_bf = sb.tile([P, Q, PACK], BF16, align_bytes=64)
+        nc.scalar.activation(qv_bf[:], qv_ps[:].rearrange("p t q -> p q t"), COPY)
+        qv_codes = sb.tile([P, Q], U32, align_bytes=64)
+        qv_plane = sb.tile([P, Q], U8, align_bytes=64)
+        nc.vector.quantize_mx(
+            out=qv_codes[:].bitcast(FP8X4), scales=qv_plane[:], in_=qv_bf[:].rearrange("p q j -> p (q j)")
+        )
+
+        a = sb.tile([P, T], F32, align_bytes=64)
+        for c, bank in enumerate(banks):
+            cols = slice(c * CHUNK, (c + 1) * CHUNK)
+            nc.tensor.matmul_mx(
+                out=bank[:],
+                lhsT=qv_codes[:].bitcast(FP8X4),
+                lhsT_scale=qv_plane[:],
+                rhs=cache_codes[:, 2 * c * CHUNK : 2 * (c + 1) * CHUNK].bitcast(FP4X4),
+                rhs_scale=cache_plane[:, cols],
+                start=False,
+                stop=True,
+            )
+            if c % 2 == 0:
+                nc.scalar.copy(a[:, cols], bank[:])
+            else:
+                nc.vector.tensor_copy(a[:, cols], bank[:])
+
+        w = sb.tile([P, I], F32, align_bytes=64)
+        nc.vector.tensor_copy(w[:, :J], a[:].indirect(l1[:]))
+        nc.scalar.activation(w[:, J:], a[:].indirect(l2[:]), COPY)
+        nc.scalar.activation(f1[:].indirect(l3[:]), w[:], COPY)
+
+        c1 = sb.tile([P, T], F32, align_bytes=64)
+        nc.vector.tensor_tensor(c1[:], a[:], f1[:], SUB)
+        v = sb.tile([P, J], F32, align_bytes=64)
+        nc.vector.tensor_tensor(v[:], c1[:].indirect(l4[:]), w[:, :J], SUB)
+        nc.scalar.activation(f2[:].indirect(l2[:]), v[:], COPY)
+        c2 = sb.tile([P, T], F32, align_bytes=64)
+        nc.vector.tensor_tensor(c2[:], c1[:], f2[:], MAX)
+
+        half = I // 2
+        y0 = sb.tile([P, half], F32, align_bytes=64)
+        y1 = sb.tile([P, half], F32, align_bytes=64)
+        nc.vector.tensor_copy(y0[:], c2[:].indirect(l5[:, : half // 16]))
+        nc.scalar.activation(y1[:], c2[:].indirect(l5[:, half // 16 :]), COPY)
+        nc.sync.dma_start(out[:, :half], y0[:])
+        nc.scalar.dma_start(out[:, half:], y1[:])

@@ -21,6 +21,8 @@ P = 128
 PACK = 4
 CHUNK = 256
 CAST_SPLIT = 64
+DEAL_SPLIT = 12
+PIECES = ((0, 256), (256, 256), (512, 256), (768, 128), (896, 128))
 
 
 def tile_attend_halfruns_parts_kernel(
@@ -43,26 +45,35 @@ def tile_attend_halfruns_parts_kernel(
                 nc.vector.tensor_copy(plane[32 * g : 32 * g + PACK, :].bitcast(I32), rows[:, g, :])
 
         wq_plane = sb.tile([P, K], U8, align_bytes=64)
-        tags_plane = sb.tile([P, T], U8, align_bytes=64)
+        tags_plane = sb.tile([P, CHUNK], U8, align_bytes=64)
         cache_plane = sb.tile([P, T], U8, align_bytes=64)
-        for plane in (wq_plane, tags_plane, cache_plane):
+        for plane in (tags_plane, cache_plane, wq_plane):
             nc.vector.memset(plane[:].bitcast(I32), 0)
         f1 = sb.tile([P, T], F32, align_bytes=64)
-        f2 = sb.tile([P, T], F32, align_bytes=64)
         nc.vector.memset(f1[:], 0.0)
-        nc.vector.memset(f2[:], 0.0)
 
         wq_rows = load_scale_rows(wq_scales, K, "wq_rows")
         st_raw = sb.tile([P, PACK, Q], F32, align_bytes=64)
         nc.sync.dma_start(st_raw[:], states.rearrange("(p j) q -> p j q", j=PACK))
         wq_raw = sb.tile([P, K], U32, align_bytes=64)
         nc.sync.dma_start(wq_raw[:].bitcast(I32), wq_words[0].rearrange("p n t -> p (n t)").bitcast(I32))
-        tags_rows = load_scale_rows(tags_scales, T, "tags_rows")
-        cache_rows = load_scale_rows(cache_scales, T, "cache_rows")
-        tags_codes = sb.tile([P, T], U32, align_bytes=64)
-        nc.sync.dma_start(tags_codes[:].bitcast(I32), tags_words[0].rearrange("p n t -> p (n t)").bitcast(I32))
+        tags_rows = tags_scales[0].bitcast(I32)
+        for g in range(4):
+            nc.sync.dma_start(
+                tags_plane[32 * g : 32 * g + 16, :].bitcast(I32),
+                tags_rows[PACK * g : PACK * (g + 1), :].rearrange("r (h n) -> h r n", h=T // CHUNK),
+            )
+        tags_src = tags_words[0].rearrange("p n t -> p (n t)").bitcast(I32)
+        tags_halves = []
+        for u in range(2):
+            codes = sb.tile([P, T // 2], U32, name="tags_codes%d" % u, align_bytes=64)
+            nc.sync.dma_start(codes[:].bitcast(I32), tags_src[:, u * T // 2 : (u + 1) * T // 2])
+            tags_halves.append(codes)
         cache_codes = sb.tile([P, 2 * T], U8, align_bytes=64)
         nc.sync.dma_start(cache_codes[:].bitcast(I32), cache_words[0].bitcast(I32))
+        cache_rows = cache_scales[0].bitcast(I32)
+        for r in range(PACK):
+            nc.sync.dma_start(cache_plane[r:P:32, :].bitcast(I32), cache_rows[r:16:PACK, :])
         l1 = lists.tile([P, J // 16], U16)
         l2 = lists.tile([P, J // 16], U16)
         l3 = lists.tile([P, I // 16], U16)
@@ -90,16 +101,17 @@ def tile_attend_halfruns_parts_kernel(
             wq_plane[:].rearrange("p (m t) -> p t m", t=PACK),
         )
         wq_dealt = sb.tile([P, K], U32, align_bytes=64)
-        nc.scalar.copy(
-            wq_dealt[:].rearrange("p (t b i) -> p b t i", t=PACK, i=4),
-            wq_raw[:].rearrange("p (b i t) -> p b t i", t=PACK, i=4),
-        )
+        deal_dst = wq_dealt[:].rearrange("p (t b i) -> p b t i", t=PACK, i=4)
+        deal_src = wq_raw[:].rearrange("p (b i t) -> p b t i", t=PACK, i=4)
+        nc.scalar.copy(deal_dst[:, :DEAL_SPLIT], deal_src[:, :DEAL_SPLIT])
 
         st_codes = sb.tile([P, Q], U32, align_bytes=64)
         st_plane = sb.tile([P, Q], U8, align_bytes=64)
         nc.vector.quantize_mx(
             out=st_codes[:].bitcast(FP8X4), scales=st_plane[:], in_=st_bf[:].rearrange("p q j -> p (q j)")
         )
+
+        nc.vector.tensor_copy(deal_dst[:, DEAL_SPLIT:].bitcast(I32), deal_src[:, DEAL_SPLIT:].bitcast(I32))
 
         qv_ps = psum.tile([P, PACK, Q], F32)
         for t in range(PACK):
@@ -114,23 +126,21 @@ def tile_attend_halfruns_parts_kernel(
                 stop=True,
             )
 
-        spread_scale_rows(tags_rows, tags_plane)
-        spread_scale_rows(cache_rows, cache_plane)
-
-        banks = [psum.tile([P, CHUNK], F32, name="bank%d" % c) for c in range(T // CHUNK)]
-        for c, bank in enumerate(banks):
-            cols = slice(c * CHUNK, (c + 1) * CHUNK)
+        banks = [psum.tile([P, n], F32, name="bank%d" % c0) for c0, n in PIECES]
+        for (c0, n), bank in zip(PIECES, banks):
+            u, u0 = divmod(c0, T // 2)
+            h, h0 = divmod(c0, CHUNK)
             nc.tensor.matmul_mx(
                 out=bank[:],
                 lhsT=st_codes[:].bitcast(FP8X4),
                 lhsT_scale=st_plane[:],
-                rhs=tags_codes[:, cols].bitcast(FP8X4),
-                rhs_scale=tags_plane[:, cols],
+                rhs=tags_halves[u][:, u0 : u0 + n].bitcast(FP8X4),
+                rhs_scale=tags_plane[PACK * h :, h0 : h0 + n],
                 start=True,
                 stop=False,
             )
 
-        qv_bf = sb.tile([P, Q, PACK], BF16, align_bytes=64)
+        qv_bf = sb.tile([P, Q, PACK], BF16, tag="qv_then_f2", align_bytes=64)
         nc.scalar.activation(qv_bf[:], qv_ps[:].rearrange("p t q -> p q t"), COPY)
         qv_codes = sb.tile([P, Q], U32, align_bytes=64)
         qv_plane = sb.tile([P, Q], U8, align_bytes=64)
@@ -138,14 +148,17 @@ def tile_attend_halfruns_parts_kernel(
             out=qv_codes[:].bitcast(FP8X4), scales=qv_plane[:], in_=qv_bf[:].rearrange("p q j -> p (q j)")
         )
 
+        f2 = sb.tile([P, T], F32, tag="qv_then_f2", align_bytes=64)
+        nc.gpsimd.memset(f2[:], 0.0)
+
         a = sb.tile([P, T], F32, align_bytes=64)
-        for c, bank in enumerate(banks):
-            cols = slice(c * CHUNK, (c + 1) * CHUNK)
+        for c, ((c0, n), bank) in enumerate(zip(PIECES, banks)):
+            cols = slice(c0, c0 + n)
             nc.tensor.matmul_mx(
                 out=bank[:],
                 lhsT=qv_codes[:].bitcast(FP8X4),
                 lhsT_scale=qv_plane[:],
-                rhs=cache_codes[:, 2 * c * CHUNK : 2 * (c + 1) * CHUNK].bitcast(FP4X4),
+                rhs=cache_codes[:, 2 * c0 : 2 * (c0 + n)].bitcast(FP4X4),
                 rhs_scale=cache_plane[:, cols],
                 start=False,
                 stop=True,

@@ -174,7 +174,9 @@ def tile_attend_halfruns_parts_kernel(
         nc.scalar.activation(f1[:].indirect(l3[:]), w[:], COPY)
 
         c1 = sb.tile([P, T], F32, align_bytes=64)
-        nc.vector.tensor_tensor(c1[:], a[:], f1[:], SUB)
+        for (c0, n), bank in zip(PIECES[:3], banks):
+            nc.vector.tensor_tensor(c1[:, c0 : c0 + n], bank[:], f1[:, c0 : c0 + n], SUB)
+        nc.gpsimd.tensor_tensor(c1[:, 768:], a[:, 768:], f1[:, 768:], SUB)
         v = sb.tile([P, J], F32, align_bytes=64)
         nc.vector.tensor_tensor(v[:], c1[:].indirect(l4[:]), w[:, :J], SUB)
         nc.scalar.activation(f2[:].indirect(l2[:]), v[:], COPY)

@@ -50,7 +50,9 @@ def tile_attend_halfruns_parts_kernel(
         for plane in (tags_plane, cache_plane, wq_plane):
             nc.vector.memset(plane[:].bitcast(I32), 0)
         f1 = sb.tile([P, T], F32, align_bytes=64)
+        f2 = sb.tile([P, T], F32, align_bytes=64)
         nc.vector.memset(f1[:], 0.0)
+        nc.vector.memset(f2[:], 0.0)
 
         wq_rows = load_scale_rows(wq_scales, K, "wq_rows")
         st_raw = sb.tile([P, PACK, Q], F32, align_bytes=64)
@@ -113,11 +115,11 @@ def tile_attend_halfruns_parts_kernel(
 
         nc.vector.tensor_copy(deal_dst[:, DEAL_SPLIT:].bitcast(I32), deal_src[:, DEAL_SPLIT:].bitcast(I32))
 
-        qv_ps = psum.tile([P, PACK, Q], F32)
+        qv_ps = [psum.tile([P, 2, Q], F32, name="qv_ps%d" % u) for u in range(2)]
         for t in range(PACK):
             cols = slice(t * P, (t + 1) * P)
             nc.tensor.matmul_mx(
-                out=qv_ps[:, t, :],
+                out=qv_ps[t // 2][:, t % 2, :],
                 lhsT=wq_dealt[:, cols].bitcast(FP8X4),
                 lhsT_scale=wq_dealt_plane[:, cols],
                 rhs=st_codes[:].bitcast(FP8X4),
@@ -126,6 +128,8 @@ def tile_attend_halfruns_parts_kernel(
                 stop=True,
             )
 
+        qv_bf = sb.tile([P, Q, PACK], BF16, align_bytes=64)
+        nc.vector.tensor_copy(qv_bf[:, :, :2], qv_ps[0][:].rearrange("p t q -> p q t"))
         banks = [psum.tile([P, n], F32, name="bank%d" % c0) for c0, n in PIECES]
         for (c0, n), bank in zip(PIECES, banks):
             u, u0 = divmod(c0, T // 2)
@@ -140,16 +144,12 @@ def tile_attend_halfruns_parts_kernel(
                 stop=False,
             )
 
-        qv_bf = sb.tile([P, Q, PACK], BF16, tag="qv_then_f2", align_bytes=64)
-        nc.scalar.activation(qv_bf[:], qv_ps[:].rearrange("p t q -> p q t"), COPY)
+        nc.scalar.activation(qv_bf[:, :, 2:], qv_ps[1][:].rearrange("p t q -> p q t"), COPY)
         qv_codes = sb.tile([P, Q], U32, align_bytes=64)
         qv_plane = sb.tile([P, Q], U8, align_bytes=64)
         nc.vector.quantize_mx(
             out=qv_codes[:].bitcast(FP8X4), scales=qv_plane[:], in_=qv_bf[:].rearrange("p q j -> p (q j)")
         )
-
-        f2 = sb.tile([P, T], F32, tag="qv_then_f2", align_bytes=64)
-        nc.gpsimd.memset(f2[:], 0.0)
 
         a = sb.tile([P, T], F32, align_bytes=64)
         for c, ((c0, n), bank) in enumerate(zip(PIECES, banks)):

from contextlib import ExitStack

import concourse.mybir as mybir

D, K, T, I, J, Q = 512, 512, 1024, 512, 256, 128
FLOPS = 2 * D * K * Q + 2 * K * T * Q + 2 * D * T * Q

F32 = mybir.dt.float32
BF16 = mybir.dt.bfloat16
I32 = mybir.dt.int32
U32 = mybir.dt.uint32
U16 = mybir.dt.uint16
U8 = mybir.dt.uint8
FP8X4 = mybir.dt.float8_e4m3fn_x4
FP4X4 = mybir.dt.float4_e2m1fn_x4
COPY = mybir.ActivationFunctionType.Copy
SUB = mybir.AluOpType.subtract
MAX = mybir.AluOpType.max

P = 128
PACK = 4
CHUNK = 256
CAST_SPLIT = 64
DEAL_SPLIT = 12
PIECES = ((0, 256), (256, 256), (512, 256), (768, 128), (896, 128))


def tile_attend_halfruns_parts_kernel(
    tc, states, wq_words, wq_scales, cache_words, cache_scales, tags_words, tags_scales,
    offs, offs2, offs3, offs4, offs5, out,
):
    nc = tc.nc
    with ExitStack() as ctx:
        lists = ctx.enter_context(tc.tile_pool(name="lists", bufs=1))
        sb = ctx.enter_context(tc.tile_pool(name="sb", bufs=1))
        psum = ctx.enter_context(tc.psum_pool(name="psum", bufs=1))

        def load_scale_rows(scales, width, name):
            rows = sb.tile([PACK, 4, width // 4], I32, name=name, align_bytes=64)
            nc.sync.dma_start(rows[:], scales[0].bitcast(I32).rearrange("(g r) n -> r g n", r=PACK))
            return rows

        def spread_scale_rows(rows, plane):
            for g in range(4):
                nc.vector.tensor_copy(plane[32 * g : 32 * g + PACK, :].bitcast(I32), rows[:, g, :])

        wq_plane = sb.tile([P, K], U8, align_bytes=64)
        tags_plane = sb.tile([P, CHUNK], U8, align_bytes=64)
        cache_plane = sb.tile([P, T], U8, align_bytes=64)
        for plane in (tags_plane, cache_plane, wq_plane):
            nc.vector.memset(plane[:].bitcast(I32), 0)
        f1 = sb.tile([P, T], F32, align_bytes=64)
        f2 = sb.tile([P, T], F32, align_bytes=64)
        nc.vector.memset(f1[:], 0.0)
        nc.vector.memset(f2[:], 0.0)

        wq_rows = load_scale_rows(wq_scales, K, "wq_rows")
        st_raw = sb.tile([P, PACK, Q], F32, align_bytes=64)
        nc.sync.dma_start(st_raw[:], states.rearrange("(p j) q -> p j q", j=PACK))
        wq_raw = sb.tile([P, K], U32, align_bytes=64)
        nc.sync.dma_start(wq_raw[:].bitcast(I32), wq_words[0].rearrange("p n t -> p (n t)").bitcast(I32))
        tags_rows = tags_scales[0].bitcast(I32)
        for g in range(4):
            nc.sync.dma_start(
                tags_plane[32 * g : 32 * g + 16, :].bitcast(I32),
                tags_rows[PACK * g : PACK * (g + 1), :].rearrange("r (h n) -> h r n", h=T // CHUNK),
            )
        tags_src = tags_words[0].rearrange("p n t -> p (n t)").bitcast(I32)
        tags_halves = []
        for u in range(2):
            codes = sb.tile([P, T // 2], U32, name="tags_codes%d" % u, align_bytes=64)
            nc.sync.dma_start(codes[:].bitcast(I32), tags_src[:, u * T // 2 : (u + 1) * T // 2])
            tags_halves.append(codes)
        cache_codes = sb.tile([P, 2 * T], U8, align_bytes=64)
        nc.sync.dma_start(cache_codes[:].bitcast(I32), cache_words[0].bitcast(I32))
        cache_rows = cache_scales[0].bitcast(I32)
        for r in range(PACK):
            nc.sync.dma_start(cache_plane[r:P:32, :].bitcast(I32), cache_rows[r:16:PACK, :])
        l1 = lists.tile([P, J // 16], U16)
        l2 = lists.tile([P, J // 16], U16)
        l3 = lists.tile([P, I // 16], U16)
        l4 = lists.tile([P, J // 16], U16)
        l5 = lists.tile([P, I // 16], U16)
        for tile_, src in ((l1, offs), (l2, offs2), (l3, offs3), (l4, offs4), (l5, offs5)):
            nc.sync.dma_start(tile_[:], src)

        spread_scale_rows(wq_rows, wq_plane)

        st_bf = sb.tile([P, Q, PACK], BF16, align_bytes=64)
        nc.scalar.activation(
            st_bf[:, CAST_SPLIT:, :].rearrange("p (c i) j -> p c j i", i=4),
            st_raw[:, :, CAST_SPLIT:].rearrange("p j (c i) -> p c j i", i=4),
            COPY,
        )
        nc.vector.tensor_copy(
            st_bf[:, :CAST_SPLIT, :].rearrange("p (c i) j -> p c j i", i=4),
            st_raw[:, :, :CAST_SPLIT].rearrange("p j (c i) -> p c j i", i=4),
        )

        wq_dealt_plane = sb.tile([P, K], U8, align_bytes=64)
        nc.vector.tensor_copy(
            wq_dealt_plane[:].rearrange("p (t m) -> p t m", t=PACK),
            wq_plane[:].rearrange("p (m t) -> p t m", t=PACK),
        )
        wq_dealt = sb.tile([P, K], U32, align_bytes=64)
        deal_dst = wq_dealt[:].rearrange("p (t b i) -> p b t i", t=PACK, i=4)
        deal_src = wq_raw[:].rearrange("p (b i t) -> p b t i", t=PACK, i=4)
        nc.scalar.copy(deal_dst[:, :DEAL_SPLIT], deal_src[:, :DEAL_SPLIT])

        st_codes = sb.tile([P, Q], U32, align_bytes=64)
        st_plane = sb.tile([P, Q], U8, align_bytes=64)
        nc.vector.quantize_mx(
            out=st_codes[:].bitcast(FP8X4), scales=st_plane[:], in_=st_bf[:].rearrange("p q j -> p (q j)")
        )

        nc.vector.tensor_copy(deal_dst[:, DEAL_SPLIT:].bitcast(I32), deal_src[:, DEAL_SPLIT:].bitcast(I32))

        qv_ps = [psum.tile([P, 2, Q], F32, name="qv_ps%d" % u) for u in range(2)]
        for t in range(PACK):
            cols = slice(t * P, (t + 1) * P)
            nc.tensor.matmul_mx(
                out=qv_ps[t // 2][:, t % 2, :],
                lhsT=wq_dealt[:, cols].bitcast(FP8X4),
                lhsT_scale=wq_dealt_plane[:, cols],
                rhs=st_codes[:].bitcast(FP8X4),
                rhs_scale=st_plane[:],
                start=True,
                stop=True,
            )

        qv_bf = sb.tile([P, Q, PACK], BF16, align_bytes=64)
        nc.vector.tensor_copy(qv_bf[:, :, :2], qv_ps[0][:].rearrange("p t q -> p q t"))
        banks = [psum.tile([P, n], F32, name="bank%d" % c0) for c0, n in PIECES]
        for (c0, n), bank in zip(PIECES, banks):
            u, u0 = divmod(c0, T // 2)
            h, h0 = divmod(c0, CHUNK)
            nc.tensor.matmul_mx(
                out=bank[:],
                lhsT=st_codes[:].bitcast(FP8X4),
                lhsT_scale=st_plane[:],
                rhs=tags_halves[u][:, u0 : u0 + n].bitcast(FP8X4),
                rhs_scale=tags_plane[PACK * h :, h0 : h0 + n],
                start=True,
                stop=False,
            )

        nc.scalar.activation(qv_bf[:, :, 2:], qv_ps[1][:].rearrange("p t q -> p q t"), COPY)
        qv_codes = sb.tile([P, Q], U32, align_bytes=64)
        qv_plane = sb.tile([P, Q], U8, align_bytes=64)
        nc.vector.quantize_mx(
            out=qv_codes[:].bitcast(FP8X4), scales=qv_plane[:], in_=qv_bf[:].rearrange("p q j -> p (q j)")
        )

        a = sb.tile([P, T], F32, align_bytes=64)
        for c, ((c0, n), bank) in enumerate(zip(PIECES, banks)):
            cols = slice(c0, c0 + n)
            nc.tensor.matmul_mx(
                out=bank[:],
                lhsT=qv_codes[:].bitcast(FP8X4),
                lhsT_scale=qv_plane[:],
                rhs=cache_codes[:, 2 * c0 : 2 * (c0 + n)].bitcast(FP4X4),
                rhs_scale=cache_plane[:, cols],
                start=False,
                stop=True,
            )
            if c % 2 == 0:
                nc.scalar.copy(a[:, cols], bank[:])
            else:
                nc.vector.tensor_copy(a[:, cols], bank[:])

        w = sb.tile([P, I], F32, align_bytes=64)
        nc.vector.tensor_copy(w[:, :J], a[:].indirect(l1[:]))
        nc.scalar.activation(w[:, J:], a[:].indirect(l2[:]), COPY)
        nc.scalar.activation(f1[:].indirect(l3[:]), w[:], COPY)

        c1 = sb.tile([P, T], F32, align_bytes=64)
        for (c0, n), bank in zip(PIECES[:3], banks):
            nc.vector.tensor_tensor(c1[:, c0 : c0 + n], bank[:], f1[:, c0 : c0 + n], SUB)
        nc.gpsimd.tensor_tensor(c1[:, 768:], a[:, 768:], f1[:, 768:], SUB)
        v = sb.tile([P, J], F32, align_bytes=64)
        nc.vector.tensor_tensor(v[:], c1[:].indirect(l4[:]), w[:, :J], SUB)
        nc.scalar.activation(f2[:].indirect(l2[:]), v[:], COPY)
        c2 = sb.tile([P, T], F32, align_bytes=64)
        nc.vector.tensor_tensor(c2[:], c1[:], f2[:], MAX)

        half = I // 2
        y0 = sb.tile([P, half], F32, align_bytes=64)
        y1 = sb.tile([P, half], F32, align_bytes=64)
        nc.vector.tensor_copy(y0[:], c2[:].indirect(l5[:, : half // 16]))
        nc.scalar.activation(y1[:], c2[:].indirect(l5[:, half // 16 :]), COPY)
        nc.sync.dma_start(out[:, :half], y0[:])
        nc.scalar.dma_start(out[:, half:], y1[:])
